import numpy as np
import ml_dtypes


def mxq(x, axis, fmt="e4m3"):
    dtype, down = {"e4m3": (ml_dtypes.float8_e4m3fn, 7), "e5m2": (ml_dtypes.float8_e5m2, 14)}[fmt]
    v = np.moveaxis(np.asarray(x, np.float32).astype(ml_dtypes.bfloat16).astype(np.float64), axis, -1)
    blocks = v.reshape(v.shape[:-1] + (-1, 32))
    amax = np.abs(blocks).max(-1, keepdims=True)
    byte = np.maximum(np.where(amax > 0, np.frexp(amax)[1] - 1 + 127, 0) - down, 1)
    scale = np.exp2(byte - 127.0)
    codes = (blocks / scale).astype(np.float32).astype(dtype).astype(np.float64)
    return np.moveaxis((codes * scale).reshape(v.shape), -1, axis)


WIDE = False


def mx_kscale(k):
    if not WIDE:
        return np.ones(k)
    levels = np.array([10, -10, 5, -5, 0])
    if k % 512:
        return np.exp2(np.random.permutation(np.resize(levels, k // 32))).repeat(32)
    a = np.empty((k // 512, 16))
    for p in range(k // 512):
        a[p, :8] = np.random.permutation(np.resize(levels, 8))
        for g in range(8):
            far = levels[np.abs(levels - a[p, g]) >= 10]
            a[p, g + 8] = far[np.random.randint(len(far))]
    return np.exp2(a.ravel()).repeat(32)


def f64(x):
    return np.asarray(x).astype(np.float64)


def striped(idx):
    return np.tile(idx.reshape(-1, 16).T, (8, 1)).astype(np.uint16)


def unstriped(offs):
    return offs[:16].T.reshape(-1).astype(np.int64)


def pack_weight(w):
    k, n = w.shape
    w = f64(np.asarray(w, np.float32).astype(ml_dtypes.bfloat16)).reshape(k // 32, 32, n)
    amax = np.abs(w).max(1)
    byte = np.clip(np.where(amax > 0, np.frexp(amax)[1] - 1 + 127 - 7, 1), 1, 254)
    scaled = (w * np.exp2(127.0 - byte)[:, None, :]).reshape(k, n).astype(np.float32)
    words = np.ascontiguousarray(scaled.reshape(k // 512, 128, 4, n).transpose(0, 1, 3, 2)).astype(ml_dtypes.float8_e4m3fn).view(np.uint8)
    return words, np.ascontiguousarray(byte.astype(np.uint8).reshape(k // 512, 16, n))


def unpack_weight(words, scales):
    g, p, n, _ = words.shape
    vals = np.ascontiguousarray(words).view(ml_dtypes.float8_e4m3fn).astype(np.float64) * np.repeat(np.exp2(scales.astype(np.float64) - 127.0), 8, axis=1)[..., None]
    return vals.transpose(0, 1, 3, 2).reshape(g * 512, n)


E2M1 = np.array([0.0, 0.5, 1.0, 1.5, 2.0, 3.0, 4.0, 6.0, -0.0, -0.5, -1.0, -1.5, -2.0, -3.0, -4.0, -6.0])


def pack_fp4(w):
    k, n = w.shape
    w = f64(np.asarray(w, np.float32).astype(ml_dtypes.bfloat16)).reshape(k // 32, 32, n)
    amax = np.abs(w).max(1)
    mant, ex = np.frexp(amax / 6.0)
    byte = np.clip(np.where(amax > 0, np.where(mant > 0.5, ex, ex - 1) + 127, 1), 1, 254)
    scaled = (w * np.exp2(127.0 - byte)[:, None, :]).reshape(k, n).astype(np.float32)
    c = np.ascontiguousarray(scaled.reshape(k // 512, 128, 4, n).transpose(0, 1, 3, 2)).astype(ml_dtypes.float4_e2m1fn).view(np.uint8) & 0xF
    words = (c[..., 0::2] | (c[..., 1::2] << 4)).reshape(k // 512, 128, 2 * n)
    return np.ascontiguousarray(words), np.ascontiguousarray(byte.astype(np.uint8).reshape(k // 512, 16, n))


def unpack_fp4(words, scales):
    g, _, n = scales.shape
    words = np.ascontiguousarray(words).reshape(g, 128, n, 2)
    nib = np.empty((g, 128, n, 4), np.uint8)
    nib[..., 0::2] = words & 0xF
    nib[..., 1::2] = words >> 4
    vals = E2M1[nib] * np.repeat(np.exp2(scales.astype(np.float64) - 127.0), 8, axis=1)[..., None]
    return vals.transpose(0, 1, 3, 2).reshape(g * 512, n)


def silu(v):
    return v / (1.0 + np.exp(-np.maximum(v, -700.0)))

def planes(y):
    n, m = y.shape
    v = y.astype(np.float32).astype(ml_dtypes.bfloat16).astype(np.float64).reshape(n // 32, 32, m)
    top = np.abs(v).max(1)
    byte = np.clip(np.where(top > 0, np.frexp(top)[1] - 1 + 127 - 7, 1), 1, 254)
    codes = (v * np.exp2(127.0 - byte)[:, None, :]).reshape(n, m).astype(np.float32).astype(ml_dtypes.float8_e4m3fn).view(np.uint8)
    words = codes.reshape(n // 512, 128, 4, m).transpose(0, 1, 3, 2)
    return np.ascontiguousarray(words), np.ascontiguousarray(byte.astype(np.uint8).reshape(n // 512, 16, m))


K, T, H, J, U = 1024, 512, 512, 512, 1024


def setup_inputs():
    n = np.random.standard_normal
    s = mx_kscale(K)[:, None]
    u = mx_kscale(H)
    r = mx_kscale(J)[:, None]
    packed_xT = pack_weight(n((K, T)) * s)
    packed_w2 = pack_fp4(n((H, H)) / np.sqrt(2 * H) / u[:, None])
    return {
        "x_words": packed_xT[0],
        "x_scales": packed_xT[1],
        "aT": (n((J, U)) * r).astype(np.float32),
        "w1": (n((K, H)) / np.sqrt(K) / s * u).astype(np.float32),
        "w3": (n((J, H)) / np.sqrt(J) / r).astype(np.float32),
        "w2_words": packed_w2[0],
        "w2_scales": packed_w2[1],
        "pos1": striped(np.random.permutation(T)),
        "pos2": striped(np.random.permutation(T)),
    }


def reference(x_words, x_scales, aT, w1, w3, w2_words, w2_scales, pos1, pos2):
    xq = unpack_weight(x_words, x_scales)
    h = silu(mxq(f64(w1), 0, "e4m3").T @ xq)
    f = mxq(f64(w3), 0, "e4m3").T @ mxq(f64(aT), 0, "e4m3")
    z = h[:, unstriped(pos1)] * f[:, :T] + h[:, unstriped(pos2)] * f[:, T:2 * T]
    out_0 = unpack_fp4(w2_words, w2_scales).T @ mxq(z, 0, "e4m3")
    return (out_0,) + planes(out_0)

@@ -1,0 +1,268 @@
+from contextlib import ExitStack
+
+import concourse.mybir as mybir
+
+K, T, H, J, D = 1024, 512, 512, 512, 2
+FLOPS = 2 * (K * H * T + J * H * D * T + H * H * T)
+
+F32 = mybir.dt.float32
+BF16 = mybir.dt.bfloat16
+I32 = mybir.dt.int32
+U32 = mybir.dt.uint32
+U16 = mybir.dt.uint16
+U8 = mybir.dt.uint8
+FP8X4 = mybir.dt.float8_e4m3fn_x4
+FP4X4 = mybir.dt.float4_e2m1fn_x4
+MULT = mybir.AluOpType.mult
+ADD = mybir.AluOpType.add
+SILU = mybir.ActivationFunctionType.Silu
+
+P = 128
+PACK = 4
+K_PASS = P * PACK
+HALF = T // 2
+QUART = T // 4
+V_SHARE = 84
+
+
+def tile_picked_wdime_none_lo_kernel(tc, x_words, x_scales, aT, w1, w3, w2_words, w2_scales, pos1, pos2, out_0, out_1, out_2):
+    nc = tc.nc
+    with ExitStack() as ctx:
+        keep = ctx.enter_context(tc.tile_pool(name="keep", bufs=1))
+        psum = ctx.enter_context(tc.psum_pool(name="psum", bufs=4))
+
+        def sb(name, shape, dtype):
+            return keep.tile(shape, dtype, name=name, align_bytes=64)
+
+        lists = [keep.tile([P, T // 16], U16, name="list%d" % d) for d in range(D)]
+
+        warm_in = sb("warm_in", [P, 1], F32)
+        warm_out = sb("warm_out", [P, 1], F32)
+        nc.vector.memset(warm_in[:], 0.0)
+
+        x_sc = sb("x_sc", [P, 2, T], U8)
+        w2_sc_raw = sb("w2_sc_raw", [P, H], U8)
+        nc.gpsimd.memset(x_sc[:].rearrange("p z c -> p (z c)").bitcast(I32), 0)
+        nc.gpsimd.memset(w2_sc_raw[:].bitcast(I32), 0)
+        for q in range(4):
+            nc.scalar.dma_start(
+                out=x_sc[32 * q : 32 * q + 4, :, :].bitcast(I32),
+                in_=x_scales[:, 4 * q : 4 * q + 4, :].rearrange("z r c -> r z c").bitcast(I32),
+            )
+
+        for q in range(4):
+            nc.scalar.dma_start(
+                out=w2_sc_raw[32 * q : 32 * q + 4, :].bitcast(I32),
+                in_=w2_scales[0, 4 * q : 4 * q + 4, :].bitcast(I32),
+            )
+        nc.scalar.activation(warm_out[:], warm_in[:], SILU)
+        w2_raw = sb("w2_raw", [P, 2 * H], U8)
+        nc.sync.dma_start(out=w2_raw[:].bitcast(I32), in_=w2_words[0].bitcast(I32))
+        a_rows = aT.rearrange("(p j) u -> p j u", j=PACK)
+        a_raw = {}
+
+        def load_a(d, half):
+            a_raw[d, half] = sb("a_raw%d%d" % (d, half), [P, PACK, HALF], F32)
+            u0 = d * T + half * HALF
+            nc.sync.dma_start(out=a_raw[d, half][:], in_=a_rows[:, :, u0 : u0 + HALF])
+
+        load_a(0, 0)
+        w3_raw = sb("w3_raw", [P, PACK, H], F32)
+        nc.sync.dma_start(out=w3_raw[:], in_=w3.rearrange("(p j) c -> p j c", j=PACK))
+        w1_raw = []
+        for g in range(2):
+            w1_raw.append(sb("w1_raw%d" % g, [P, PACK, H], F32))
+            nc.sync.dma_start(out=w1_raw[g][:], in_=w1[g * K_PASS : (g + 1) * K_PASS, :].rearrange("(p j) c -> p j c", j=PACK))
+        x_codes = []
+        for g in range(2):
+            x_codes.append(sb("x_codes%d" % g, [P, T], U32))
+            nc.sync.dma_start(out=x_codes[g][:].bitcast(I32), in_=x_words[g].rearrange("p n t -> p (n t)").bitcast(I32))
+        nc.sync.dma_start(lists[0][:], pos1)
+        load_a(1, 0)
+        nc.sync.dma_start(lists[1][:], pos2)
+        load_a(0, 1)
+        load_a(1, 1)
+
+        w2_codes = sb("w2_codes", [P, 2 * H], U8)
+        nc.vector.tensor_copy(
+            out=w2_codes[:].rearrange("p (t m b) -> p m t b", t=PACK, b=2),
+            in_=w2_raw[:].rearrange("p (m t b) -> p m t b", t=PACK, b=2),
+        )
+
+        w2_sc = sb("w2_sc", [P, H], U8)
+        nc.vector.tensor_copy(
+            out=w2_sc[:].rearrange("p (t m) -> p m t", t=PACK),
+            in_=w2_sc_raw[:].rearrange("p (m t) -> p m t", t=PACK),
+        )
+
+        def cast_a(d, half, copy):
+            grouped = sb("a_bf%d%d" % (d, half), [P, HALF * PACK], BF16)
+            copy(
+                out=grouped[:].rearrange("p (c i j) -> p c j i", i=4, j=PACK),
+                in_=a_raw[d, half][:].rearrange("p j (c i) -> p c j i", i=4),
+            )
+            return grouped
+
+        def quantise(name, grouped, width):
+            codes = sb(name + "_codes", [P, width], U32)
+            scales = sb(name + "_scales", [P, width], U8)
+            nc.vector.quantize_mx(out=codes[:].bitcast(FP8X4), scales=scales[:], in_=grouped[:])
+            return codes, scales
+
+        def cast_w(name, raw):
+            grouped = sb(name + "_bf", [P, H * PACK], BF16)
+            dst = grouped[:].rearrange("p (t m j) -> p m j t", t=PACK, j=PACK)
+            src = raw[:].rearrange("p j (m t) -> p m j t", t=PACK)
+            nc.vector.tensor_copy(out=dst[:, :V_SHARE], in_=src[:, :V_SHARE])
+            nc.scalar.copy(out=dst[:, V_SHARE:], in_=src[:, V_SHARE:])
+            return grouped
+
+        filt = {}
+
+        def filters(d, half, a_q):
+            for pair in range(2):
+                bank = psum.tile([P, 2, HALF], F32, name="f_bank", tag="f_bank")
+                for e in range(2):
+                    cols = slice((2 * pair + e) * P, (2 * pair + e + 1) * P)
+                    nc.tensor.matmul_mx(
+                        out=bank[:, e, :],
+                        lhsT=w3_q[0][:, cols].bitcast(FP8X4),
+                        lhsT_scale=w3_q[1][:, cols],
+                        rhs=a_q[0][:].bitcast(FP8X4),
+                        rhs_scale=a_q[1][:],
+                        start=True,
+                        stop=True,
+                    )
+                filt[d, half, pair] = sb("filt%d%d%d" % (d, half, pair), [P, 2, HALF], F32)
+                nc.scalar.copy(out=filt[d, half, pair][:], in_=bank[:])
+
+        a00_q = quantise("a00", cast_a(0, 0, nc.vector.tensor_copy), HALF)
+        w3_q = quantise("w3", cast_w("w3", w3_raw), H)
+        filters(0, 0, a00_q)
+        w1_q = [quantise("w1%d" % g, cast_w("w1%d" % g, w1_raw[g]), H) for g in range(2)]
+
+        hidden = []
+        for t in range(PACK):
+            cols = slice(t * P, (t + 1) * P)
+            bank = psum.tile([P, T], F32, name="wide_bank", tag="wide_bank")
+            for g in range(2):
+                nc.tensor.matmul_mx(
+                    out=bank[:],
+                    lhsT=w1_q[g][0][:, cols].bitcast(FP8X4),
+                    lhsT_scale=w1_q[g][1][:, cols],
+                    rhs=x_codes[g][:].bitcast(FP8X4),
+                    rhs_scale=x_sc[:, g, :],
+                    start=(g == 0),
+                    stop=(g == 1),
+                )
+            hidden.append(sb("hidden%d" % t, [P, T], F32))
+            nc.scalar.activation(hidden[t][:], bank[:], SILU)
+
+        def gather(d, t, v0, width, dst):
+            half, off = divmod(v0, HALF)
+            nc.vector.tensor_tensor(
+                dst[:, t, :],
+                hidden[t][:].indirect(lists[d][:, v0 // 16 : (v0 + width) // 16]),
+                filt[d, half, t // 2][:, t % 2, off : off + width],
+                MULT,
+            )
+
+        def add_terms(name, first, second, width):
+            grouped = sb(name, [P, width * PACK], BF16)
+            nc.vector.tensor_tensor(
+                grouped[:].rearrange("p (c i t) -> p c t i", i=4, t=PACK),
+                first.rearrange("p t (c i) -> p c t i", i=4),
+                second.rearrange("p t (c i) -> p c t i", i=4),
+                ADD,
+            )
+            return grouped
+
+        y_codes = sb("y_codes", [P, T], U32)
+        y_scales = sb("y_scales", [P, T], U8)
+        out_rows = out_0.rearrange("(p t) v -> p t v", t=PACK)
+        out_words = out_1[0].rearrange("p n t -> p (n t)").bitcast(I32)
+
+        def project(z_q, off, dst, t):
+            nc.tensor.matmul_mx(
+                out=dst,
+                lhsT=w2_codes[:, 2 * P * t : 2 * P * (t + 1)].bitcast(FP4X4),
+                lhsT_scale=w2_sc[:, P * t : P * (t + 1)],
+                rhs=z_q[0][:, off : off + QUART].bitcast(FP8X4),
+                rhs_scale=z_q[1][:, off : off + QUART],
+                start=True,
+                stop=True,
+            )
+
+        def quantise_y(grouped, v0, width):
+            cols = slice(v0, v0 + width)
+            nc.vector.quantize_mx(out=y_codes[:, cols].bitcast(FP8X4), scales=y_scales[:, cols], in_=grouped[:])
+            nc.sync.dma_start(out=out_words[:, cols], in_=y_codes[:, cols].bitcast(I32))
+
+        def finish_scalar(z_q, off, v0, y_bf):
+            bank = psum.tile([P, PACK, QUART], F32, name="wide_bank", tag="wide_bank")
+            for t in range(PACK):
+                project(z_q, off, bank[:, t, :], t)
+            y = sb("y%d" % v0, [P, PACK, QUART], F32)
+            nc.scalar.copy(out=y[:], in_=bank[:])
+            nc.sync.dma_start(out=out_rows[:, :, v0 : v0 + QUART], in_=y[:])
+            nc.scalar.copy(out=y_bf.rearrange("p (v t) -> p v t", t=PACK), in_=bank[:].rearrange("p t v -> p v t"))
+
+        a10_q = quantise("a10", cast_a(1, 0, nc.vector.tensor_copy), HALF)
+        filters(1, 0, a10_q)
+        term = {}
+        for d in range(D):
+            term[d, 0] = sb("term%d0" % d, [P, PACK, HALF], F32)
+        for t in range(PACK):
+            gather(0, t, 0, HALF, term[0, 0])
+        a01_bf = cast_a(0, 1, nc.scalar.copy)
+        gather(1, 0, 0, HALF, term[1, 0])
+        gather(1, 1, 0, HALF, term[1, 0])
+        filters(0, 1, quantise("a01", a01_bf, HALF))
+        a11_bf = cast_a(1, 1, nc.scalar.copy)
+        gather(1, 2, 0, HALF, term[1, 0])
+        gather(1, 3, 0, HALF, term[1, 0])
+        z0_bf = add_terms("z0_bf", term[0, 0][:], term[1, 0][:], HALF)
+        filters(1, 1, quantise("a11", a11_bf, HALF))
+        z0_q = quantise("z0", z0_bf, HALF)
+
+        term[0, 1] = sb("term01", [P, PACK, HALF], F32)
+        for t in range(PACK):
+            gather(0, t, HALF, HALF, term[0, 1])
+        y0_bf = sb("y0_bf", [P, HALF * PACK], BF16)
+        for k in range(2):
+            finish_scalar(z0_q, k * QUART, k * QUART, y0_bf[:, k * QUART * PACK : (k + 1) * QUART * PACK])
+        term2 = sb("term12", [P, PACK, QUART], F32)
+        term3 = sb("term13", [P, PACK, QUART], F32)
+        for t in range(PACK):
+            gather(1, t, 2 * QUART, QUART, term2)
+        gather(1, 0, 3 * QUART, QUART, term3)
+        z2_bf = add_terms("z2_bf", term[0, 1][:, :, :QUART], term2[:], QUART)
+        gather(1, 1, 3 * QUART, QUART, term3)
+        z2_q = quantise("z2", z2_bf, QUART)
+        gather(1, 2, 3 * QUART, QUART, term3)
+        gather(1, 3, 3 * QUART, QUART, term3)
+        quantise_y(y0_bf, 0, HALF)
+        z3_bf = add_terms("z3_bf", term[0, 1][:, :, QUART:], term3[:], QUART)
+        y2_bf = sb("y2_bf", [P, QUART * PACK], BF16)
+        finish_scalar(z2_q, 0, 2 * QUART, y2_bf[:])
+        z3_q = quantise("z3", z3_bf, QUART)
+        quantise_y(y2_bf, 2 * QUART, QUART)
+
+        y3 = sb("y3", [P, PACK, QUART], F32)
+        for pair, copy in enumerate((nc.vector.tensor_copy, nc.scalar.copy)):
+            bank = psum.tile([P, 2, QUART], F32, name="f_bank", tag="f_bank")
+            for e in range(2):
+                project(z3_q, 0, bank[:, e, :], 2 * pair + e)
+            copy(out=y3[:, 2 * pair : 2 * pair + 2, :], in_=bank[:])
+        nc.sync.dma_start(out=out_rows[:, :, 3 * QUART :], in_=y3[:])
+        y3_bf = sb("y3_bf", [P, QUART * PACK], BF16)
+        nc.vector.tensor_copy(
+            out=y3_bf[:].rearrange("p (c i t) -> p c t i", i=4, t=PACK),
+            in_=y3[:].rearrange("p t (c i) -> p c t i", i=4),
+        )
+        quantise_y(y3_bf, 3 * QUART, QUART)
+        for q, queue in enumerate((nc.scalar, nc.sync, nc.scalar, nc.sync)):
+            queue.dma_start(
+                out=out_2[0, 4 * q : 4 * q + 4, :].bitcast(I32),
+                in_=y_scales[32 * q : 32 * q + 4, :].bitcast(I32),
+            )

@@ -29,10 +29,10 @@ def tile_picked_wdime_none_lo_kernel(tc, x_words, x_scales, aT, w1, w3, w2_words
     nc = tc.nc
     with ExitStack() as ctx:
         keep = ctx.enter_context(tc.tile_pool(name="keep", bufs=1))
-        psum = ctx.enter_context(tc.psum_pool(name="psum", bufs=4))
+        psum = ctx.enter_context(tc.psum_pool(name="psum", bufs=1))
 
-        def sb(name, shape, dtype):
-            return keep.tile(shape, dtype, name=name, align_bytes=64)
+        def sb(name, shape, dtype, tag=None):
+            return keep.tile(shape, dtype, name=name, tag=tag or name, align_bytes=64)
 
         lists = [keep.tile([P, T // 16], U16, name="list%d" % d) for d in range(D)]
 
@@ -40,48 +40,45 @@ def tile_picked_wdime_none_lo_kernel(tc, x_words, x_scales, aT, w1, w3, w2_words
         warm_out = sb("warm_out", [P, 1], F32)
         nc.vector.memset(warm_in[:], 0.0)
 
-        x_sc = sb("x_sc", [P, 2, T], U8)
+        x_sc = sb("x_sc", [P, T], U8)
         w2_sc_raw = sb("w2_sc_raw", [P, H], U8)
-        nc.gpsimd.memset(x_sc[:].rearrange("p z c -> p (z c)").bitcast(I32), 0)
+        nc.gpsimd.memset(x_sc[:].bitcast(I32), 0)
         nc.gpsimd.memset(w2_sc_raw[:].bitcast(I32), 0)
-        for q in range(4):
-            nc.scalar.dma_start(
-                out=x_sc[32 * q : 32 * q + 4, :, :].bitcast(I32),
-                in_=x_scales[:, 4 * q : 4 * q + 4, :].rearrange("z r c -> r z c").bitcast(I32),
-            )
-
-        for q in range(4):
-            nc.scalar.dma_start(
-                out=w2_sc_raw[32 * q : 32 * q + 4, :].bitcast(I32),
-                in_=w2_scales[0, 4 * q : 4 * q + 4, :].bitcast(I32),
-            )
         nc.scalar.activation(warm_out[:], warm_in[:], SILU)
         w2_raw = sb("w2_raw", [P, 2 * H], U8)
         nc.sync.dma_start(out=w2_raw[:].bitcast(I32), in_=w2_words[0].bitcast(I32))
-        a_rows = aT.rearrange("(p j) u -> p j u", j=PACK)
-        a_raw = {}
-
-        def load_a(d, half):
-            a_raw[d, half] = sb("a_raw%d%d" % (d, half), [P, PACK, HALF], F32)
-            u0 = d * T + half * HALF
-            nc.sync.dma_start(out=a_raw[d, half][:], in_=a_rows[:, :, u0 : u0 + HALF])
-
-        load_a(0, 0)
+        a_rows = aT.rearrange("(p j) (d v) -> p j d v", j=PACK, d=D)
+        a_first = sb("a_first", [P, PACK * D, HALF], F32)
+        nc.sync.dma_start(out=a_first[:], in_=aT.rearrange("(p j) (d v) -> p (j d) v", j=PACK, d=D)[:, :, :HALF])
+        for q in range(4):
+            nc.sync.dma_start(
+                out=x_sc[32 * q : 32 * q + 8, :].bitcast(I32),
+                in_=x_scales[:, 4 * q : 4 * q + 4, :].bitcast(I32),
+            )
         w3_raw = sb("w3_raw", [P, PACK, H], F32)
         nc.sync.dma_start(out=w3_raw[:], in_=w3.rearrange("(p j) c -> p j c", j=PACK))
-        w1_raw = []
-        for g in range(2):
-            w1_raw.append(sb("w1_raw%d" % g, [P, PACK, H], F32))
-            nc.sync.dma_start(out=w1_raw[g][:], in_=w1[g * K_PASS : (g + 1) * K_PASS, :].rearrange("(p j) c -> p j c", j=PACK))
+        w1_rows = w1.rearrange("(g p j) c -> g p j c", g=2, j=PACK)
+        w10_raw = sb("w10_raw", [P, PACK, H], F32)
+        nc.sync.dma_start(out=w10_raw[:], in_=w1_rows[0])
+        w11_raw = []
+        for s in range(2):
+            w11_raw.append(sb("w11_raw%d" % s, [P, PACK, H // 2], F32))
+            nc.sync.dma_start(out=w11_raw[s][:], in_=w1_rows[1][:, :, s * (H // 2) : (s + 1) * (H // 2)])
         x_codes = []
         for g in range(2):
             x_codes.append(sb("x_codes%d" % g, [P, T], U32))
             nc.sync.dma_start(out=x_codes[g][:].bitcast(I32), in_=x_words[g].rearrange("p n t -> p (n t)").bitcast(I32))
         nc.sync.dma_start(lists[0][:], pos1)
-        load_a(1, 0)
         nc.sync.dma_start(lists[1][:], pos2)
-        load_a(0, 1)
-        load_a(1, 1)
+        a_raw = []
+        for d in range(D):
+            a_raw.append(sb("a_raw%d" % d, [P, PACK, HALF], F32))
+            nc.sync.dma_start(out=a_raw[d][:], in_=a_rows[:, :, d, HALF:])
+        for q in range(4):
+            nc.sync.dma_start(
+                out=w2_sc_raw[32 * q : 32 * q + 4, :].bitcast(I32),
+                in_=w2_scales[0, 4 * q : 4 * q + 4, :].bitcast(I32),
+            )
 
         w2_codes = sb("w2_codes", [P, 2 * H], U8)
         nc.vector.tensor_copy(
@@ -89,86 +86,105 @@ def tile_picked_wdime_none_lo_kernel(tc, x_words, x_scales, aT, w1, w3, w2_words
             in_=w2_raw[:].rearrange("p (m t b) -> p m t b", t=PACK, b=2),
         )
 
-        w2_sc = sb("w2_sc", [P, H], U8)
-        nc.vector.tensor_copy(
-            out=w2_sc[:].rearrange("p (t m) -> p m t", t=PACK),
-            in_=w2_sc_raw[:].rearrange("p (m t) -> p m t", t=PACK),
-        )
-
-        def cast_a(d, half, copy):
-            grouped = sb("a_bf%d%d" % (d, half), [P, HALF * PACK], BF16)
+        def cast_a(name, raw, width, copy, tag=None):
+            grouped = sb(name, [P, width * PACK], BF16, tag)
             copy(
                 out=grouped[:].rearrange("p (c i j) -> p c j i", i=4, j=PACK),
-                in_=a_raw[d, half][:].rearrange("p j (c i) -> p c j i", i=4),
+                in_=raw.rearrange("p j (c i) -> p c j i", i=4),
             )
             return grouped
 
         def quantise(name, grouped, width):
             codes = sb(name + "_codes", [P, width], U32)
             scales = sb(name + "_scales", [P, width], U8)
-            nc.vector.quantize_mx(out=codes[:].bitcast(FP8X4), scales=scales[:], in_=grouped[:])
+            nc.vector.quantize_mx(out=codes[:].bitcast(FP8X4), scales=scales[:], in_=grouped)
             return codes, scales
 
-        def cast_w(name, raw):
-            grouped = sb(name + "_bf", [P, H * PACK], BF16)
-            dst = grouped[:].rearrange("p (t m j) -> p m j t", t=PACK, j=PACK)
+        def cast_w(grouped, raw, m0, count):
+            dst = grouped[:].rearrange("p (t m j) -> p m j t", t=PACK, j=PACK)[:, m0 : m0 + count]
             src = raw[:].rearrange("p j (m t) -> p m j t", t=PACK)
-            nc.vector.tensor_copy(out=dst[:, :V_SHARE], in_=src[:, :V_SHARE])
-            nc.scalar.copy(out=dst[:, V_SHARE:], in_=src[:, V_SHARE:])
-            return grouped
+            share = count * V_SHARE // P // 4 * 4
+            nc.vector.tensor_copy(out=dst[:, :share], in_=src[:, :share])
+            nc.scalar.copy(out=dst[:, share:], in_=src[:, share:])
 
         filt = {}
 
-        def filters(d, half, a_q):
-            for pair in range(2):
-                bank = psum.tile([P, 2, HALF], F32, name="f_bank", tag="f_bank")
-                for e in range(2):
-                    cols = slice((2 * pair + e) * P, (2 * pair + e + 1) * P)
-                    nc.tensor.matmul_mx(
-                        out=bank[:, e, :],
-                        lhsT=w3_q[0][:, cols].bitcast(FP8X4),
-                        lhsT_scale=w3_q[1][:, cols],
-                        rhs=a_q[0][:].bitcast(FP8X4),
-                        rhs_scale=a_q[1][:],
-                        start=True,
-                        stop=True,
-                    )
-                filt[d, half, pair] = sb("filt%d%d%d" % (d, half, pair), [P, 2, HALF], F32)
-                nc.scalar.copy(out=filt[d, half, pair][:], in_=bank[:])
+        def filter_product(dst, t, a_q):
+            cols = slice(t * P, (t + 1) * P)
+            nc.tensor.matmul_mx(
+                out=dst,
+                lhsT=w3_q[0][:, cols].bitcast(FP8X4),
+                lhsT_scale=w3_q[1][:, cols],
+                rhs=a_q[0][:].bitcast(FP8X4),
+                rhs_scale=a_q[1][:],
+                start=True,
+                stop=True,
+            )
 
-        a00_q = quantise("a00", cast_a(0, 0, nc.vector.tensor_copy), HALF)
-        w3_q = quantise("w3", cast_w("w3", w3_raw), H)
-        filters(0, 0, a00_q)
-        w1_q = [quantise("w1%d" % g, cast_w("w1%d" % g, w1_raw[g]), H) for g in range(2)]
+        def late_filters(d, a_q):
+            for pair in range(2):
+                bank = psum.tile([P, 2, HALF], F32, name="f_bank", tag="b%d" % (2 * d + pair))
+                for e in range(2):
+                    filter_product(bank[:, e, :], 2 * pair + e, a_q)
+                both = sb("filt_late%d%d" % (d, pair), [P, 2, HALF], F32)
+                nc.scalar.copy(out=both[:], in_=bank[:])
+                for e in range(2):
+                    filt[d, 1, 2 * pair + e] = both[:, e, :]
+
+        a_first_bf = cast_a("a_first_bf", a_first[:].rearrange("p (j d) v -> p j (d v)", d=D), T, nc.vector.tensor_copy)
+        a_first_q = quantise("a_first", a_first_bf[:], T)
+        w3_bf = sb("w3_bf", [P, H * PACK], BF16)
+        cast_w(w3_bf, w3_raw, 0, P)
+        w3_q = quantise("w3", w3_bf[:], H)
+        f_banks = []
+        for t in range(PACK):
+            f_banks.append(psum.tile([P, T], F32, name="f_first", tag="b%d" % t))
+            filter_product(f_banks[t][:], t, a_first_q)
+        w10_bf = sb("w10_bf", [P, H * PACK], BF16)
+        cast_w(w10_bf, w10_raw, 0, P)
+        w10_q = quantise("w10", w10_bf[:], H)
+        w11_bf = sb("w11_bf", [P, H * PACK], BF16, "w10_bf")
+        for s in range(2):
+            cast_w(w11_bf, w11_raw[s], s * (P // 2), P // 2)
+        w11_q = [quantise("w11%d" % u, w11_bf[:, u * 2 * K_PASS : (u + 1) * 2 * K_PASS], 2 * P) for u in range(2)]
 
         hidden = []
         for t in range(PACK):
-            cols = slice(t * P, (t + 1) * P)
-            bank = psum.tile([P, T], F32, name="wide_bank", tag="wide_bank")
-            for g in range(2):
+            both = sb("filt_first%d" % t, [P, D, HALF], F32)
+            nc.scalar.copy(out=both[:].rearrange("p d v -> p (d v)"), in_=f_banks[t][:])
+            for d in range(D):
+                filt[d, 0, t] = both[:, d, :]
+            bank = psum.tile([P, T], F32, name="h_bank", tag="b%d" % (4 + t))
+            stationary = ((w10_q, slice(t * P, (t + 1) * P)), (w11_q[t // 2], slice(t % 2 * P, (t % 2 + 1) * P)))
+            order = (0, 1) if t == 0 else (1, 0)
+            for g in order:
+                w_q, cols = stationary[g]
                 nc.tensor.matmul_mx(
                     out=bank[:],
-                    lhsT=w1_q[g][0][:, cols].bitcast(FP8X4),
-                    lhsT_scale=w1_q[g][1][:, cols],
+                    lhsT=w_q[0][:, cols].bitcast(FP8X4),
+                    lhsT_scale=w_q[1][:, cols],
                     rhs=x_codes[g][:].bitcast(FP8X4),
-                    rhs_scale=x_sc[:, g, :],
-                    start=(g == 0),
-                    stop=(g == 1),
+                    rhs_scale=x_sc[4 * g :, :],
+                    start=(g == order[0]),
+                    stop=(g == order[1]),
                 )
             hidden.append(sb("hidden%d" % t, [P, T], F32))
             nc.scalar.activation(hidden[t][:], bank[:], SILU)
+
+        probe = sb("probe", [P, 2], F32)
+        nc.gpsimd.tensor_copy(out=probe[:, 0:1], in_=hidden[0][:, 0:1])
 
         def gather(d, t, v0, width, dst):
             half, off = divmod(v0, HALF)
             nc.vector.tensor_tensor(
                 dst[:, t, :],
                 hidden[t][:].indirect(lists[d][:, v0 // 16 : (v0 + width) // 16]),
-                filt[d, half, t // 2][:, t % 2, off : off + width],
+                filt[d, half, t][:, off : off + width],
                 MULT,
             )
 
-        def add_terms(name, first, second, width):
-            grouped = sb(name, [P, width * PACK], BF16)
+        def add_terms(name, first, second, width, tag=None):
+            grouped = sb(name, [P, width * PACK], BF16, tag)
             nc.vector.tensor_tensor(
                 grouped[:].rearrange("p (c i t) -> p c t i", i=4, t=PACK),
                 first.rearrange("p t (c i) -> p c t i", i=4),
@@ -198,8 +214,8 @@ def tile_picked_wdime_none_lo_kernel(tc, x_words, x_scales, aT, w1, w3, w2_words
             nc.vector.quantize_mx(out=y_codes[:, cols].bitcast(FP8X4), scales=y_scales[:, cols], in_=grouped[:])
             nc.sync.dma_start(out=out_words[:, cols], in_=y_codes[:, cols].bitcast(I32))
 
-        def finish_scalar(z_q, off, v0, y_bf):
-            bank = psum.tile([P, PACK, QUART], F32, name="wide_bank", tag="wide_bank")
+        def finish_scalar(z_q, off, v0, y_bf, tag):
+            bank = psum.tile([P, PACK, QUART], F32, name="y_bank", tag=tag)
             for t in range(PACK):
                 project(z_q, off, bank[:, t, :], t)
             y = sb("y%d" % v0, [P, PACK, QUART], F32)
@@ -207,30 +223,32 @@ def tile_picked_wdime_none_lo_kernel(tc, x_words, x_scales, aT, w1, w3, w2_words
             nc.sync.dma_start(out=out_rows[:, :, v0 : v0 + QUART], in_=y[:])
             nc.scalar.copy(out=y_bf.rearrange("p (v t) -> p v t", t=PACK), in_=bank[:].rearrange("p t v -> p v t"))
 
-        a10_q = quantise("a10", cast_a(1, 0, nc.vector.tensor_copy), HALF)
-        filters(1, 0, a10_q)
         term = {}
         for d in range(D):
             term[d, 0] = sb("term%d0" % d, [P, PACK, HALF], F32)
         for t in range(PACK):
-            gather(0, t, 0, HALF, term[0, 0])
-        a01_bf = cast_a(0, 1, nc.scalar.copy)
-        gather(1, 0, 0, HALF, term[1, 0])
-        gather(1, 1, 0, HALF, term[1, 0])
-        filters(0, 1, quantise("a01", a01_bf, HALF))
-        a11_bf = cast_a(1, 1, nc.scalar.copy)
-        gather(1, 2, 0, HALF, term[1, 0])
-        gather(1, 3, 0, HALF, term[1, 0])
-        z0_bf = add_terms("z0_bf", term[0, 0][:], term[1, 0][:], HALF)
-        filters(1, 1, quantise("a11", a11_bf, HALF))
-        z0_q = quantise("z0", z0_bf, HALF)
+            for d in range(D):
+                gather(d, t, 0, HALF, term[d, 0])
+        a0_bf = cast_a("a0_bf", a_raw[0][:], HALF, nc.scalar.copy, "w111_codes")
+        late_filters(0, quantise("a0", a0_bf[:], HALF))
+        a1_bf = cast_a("a1_bf", a_raw[1][:], HALF, nc.scalar.copy, "a_raw0")
+        z0_bf = add_terms("z0_bf", term[0, 0][:], term[1, 0][:], HALF, "w111_codes")
+        late_filters(1, quantise("a1", a1_bf[:], HALF))
+        w2_sc = sb("w2_sc", [P, H], U8, "filt_first3")
+        nc.vector.tensor_copy(
+            out=w2_sc[:].rearrange("p (t m) -> p m t", t=PACK),
+            in_=w2_sc_raw[:].rearrange("p (m t) -> p m t", t=PACK),
+        )
+        z0_q = quantise("z0", z0_bf[:], HALF)
 
+        probe2 = sb("probe2", [P, 2], U32)
+        nc.gpsimd.tensor_copy(out=probe2[:, 0:1], in_=z0_q[0][:, 0:1])
         term[0, 1] = sb("term01", [P, PACK, HALF], F32)
         for t in range(PACK):
             gather(0, t, HALF, HALF, term[0, 1])
         y0_bf = sb("y0_bf", [P, HALF * PACK], BF16)
         for k in range(2):
-            finish_scalar(z0_q, k * QUART, k * QUART, y0_bf[:, k * QUART * PACK : (k + 1) * QUART * PACK])
+            finish_scalar(z0_q, k * QUART, k * QUART, y0_bf[:, k * QUART * PACK : (k + 1) * QUART * PACK], "b%d" % (2 + k))
         term2 = sb("term12", [P, PACK, QUART], F32)
         term3 = sb("term13", [P, PACK, QUART], F32)
         for t in range(PACK):
@@ -238,19 +256,19 @@ def tile_picked_wdime_none_lo_kernel(tc, x_words, x_scales, aT, w1, w3, w2_words
         gather(1, 0, 3 * QUART, QUART, term3)
         z2_bf = add_terms("z2_bf", term[0, 1][:, :, :QUART], term2[:], QUART)
         gather(1, 1, 3 * QUART, QUART, term3)
-        z2_q = quantise("z2", z2_bf, QUART)
+        z2_q = quantise("z2", z2_bf[:], QUART)
         gather(1, 2, 3 * QUART, QUART, term3)
         gather(1, 3, 3 * QUART, QUART, term3)
         quantise_y(y0_bf, 0, HALF)
         z3_bf = add_terms("z3_bf", term[0, 1][:, :, QUART:], term3[:], QUART)
         y2_bf = sb("y2_bf", [P, QUART * PACK], BF16)
-        finish_scalar(z2_q, 0, 2 * QUART, y2_bf[:])
-        z3_q = quantise("z3", z3_bf, QUART)
+        finish_scalar(z2_q, 0, 2 * QUART, y2_bf[:], "b4")
+        z3_q = quantise("z3", z3_bf[:], QUART)
         quantise_y(y2_bf, 2 * QUART, QUART)
 
         y3 = sb("y3", [P, PACK, QUART], F32)
         for pair, copy in enumerate((nc.vector.tensor_copy, nc.scalar.copy)):
-            bank = psum.tile([P, 2, QUART], F32, name="f_bank", tag="f_bank")
+            bank = psum.tile([P, 2, QUART], F32, name="last_bank", tag="b%d" % (5 + pair))
             for e in range(2):
                 project(z3_q, 0, bank[:, e, :], 2 * pair + e)
             copy(out=y3[:, 2 * pair : 2 * pair + 2, :], in_=bank[:])

@@ -20,9 +20,11 @@ SILU = mybir.ActivationFunctionType.Silu
 P = 128
 PACK = 4
 K_PASS = P * PACK
+QUADRANTS = 4
 HALF = T // 2
-QUART = T // 4
-V_SHARE = 84
+QUARTER = T // 4
+LINE = 4
+W3_ON_VECTOR = 84
 
 
 def tile_picked_wdime_none_lo_kernel(tc, x_words, x_scales, aT, w1, w3, w2_words, w2_scales, pos1, pos2, out_0, out_1, out_2):
@@ -31,54 +33,58 @@ def tile_picked_wdime_none_lo_kernel(tc, x_words, x_scales, aT, w1, w3, w2_words
         keep = ctx.enter_context(tc.tile_pool(name="keep", bufs=1))
         psum = ctx.enter_context(tc.psum_pool(name="psum", bufs=1))
 
-        def sb(name, shape, dtype, tag=None):
-            return keep.tile(shape, dtype, name=name, tag=tag or name, align_bytes=64)
+        def sb(name, shape, dtype, bytes_of=None):
+            return keep.tile(shape, dtype, name=name, tag=bytes_of or name, align_bytes=64)
+
+        def bank_tile(name, shape, number):
+            return psum.tile(shape, F32, name=name, tag="bank%d" % number)
 
         lists = [keep.tile([P, T // 16], U16, name="list%d" % d) for d in range(D)]
 
-        warm_in = sb("warm_in", [P, 1], F32)
-        warm_out = sb("warm_out", [P, 1], F32)
-        nc.vector.memset(warm_in[:], 0.0)
+        zero = sb("zero", [P, 1], F32)
+        zero_bias = sb("zero_bias", [P, 1], F32)
+        nc.vector.memset(zero[:], 0.0)
 
-        x_sc = sb("x_sc", [P, T], U8)
-        w2_sc_raw = sb("w2_sc_raw", [P, H], U8)
-        nc.gpsimd.memset(x_sc[:].bitcast(I32), 0)
-        nc.gpsimd.memset(w2_sc_raw[:].bitcast(I32), 0)
-        nc.scalar.activation(warm_out[:], warm_in[:], SILU)
+        x_scale_rows = sb("x_scale_rows", [P, T], U8)
+        w2_scale_rows = sb("w2_scale_rows", [P, H], U8)
+        nc.gpsimd.memset(w2_scale_rows[:].bitcast(I32), 0)
+        nc.gpsimd.memset(x_scale_rows[:].bitcast(I32), 0)
+        nc.scalar.activation(zero_bias[:], zero[:], SILU)
+
         w2_raw = sb("w2_raw", [P, 2 * H], U8)
         nc.sync.dma_start(out=w2_raw[:].bitcast(I32), in_=w2_words[0].bitcast(I32))
-        a_rows = aT.rearrange("(p j) (d v) -> p j d v", j=PACK, d=D)
         a_first = sb("a_first", [P, PACK * D, HALF], F32)
         nc.sync.dma_start(out=a_first[:], in_=aT.rearrange("(p j) (d v) -> p (j d) v", j=PACK, d=D)[:, :, :HALF])
-        for q in range(4):
+        for q in range(QUADRANTS):
             nc.sync.dma_start(
-                out=x_sc[32 * q : 32 * q + 8, :].bitcast(I32),
-                in_=x_scales[:, 4 * q : 4 * q + 4, :].bitcast(I32),
+                out=w2_scale_rows[32 * q : 32 * q + 4, :].bitcast(I32),
+                in_=w2_scales[0, 4 * q : 4 * q + 4, :].bitcast(I32),
             )
         w3_raw = sb("w3_raw", [P, PACK, H], F32)
         nc.sync.dma_start(out=w3_raw[:], in_=w3.rearrange("(p j) c -> p j c", j=PACK))
         w1_rows = w1.rearrange("(g p j) c -> g p j c", g=2, j=PACK)
-        w10_raw = sb("w10_raw", [P, PACK, H], F32)
-        nc.sync.dma_start(out=w10_raw[:], in_=w1_rows[0])
-        w11_raw = []
+        w1_pass0_raw = sb("w1_pass0_raw", [P, PACK, H], F32)
+        nc.sync.dma_start(out=w1_pass0_raw[:], in_=w1_rows[0])
+        for q in range(QUADRANTS):
+            nc.sync.dma_start(
+                out=x_scale_rows[32 * q : 32 * q + 8, :].bitcast(I32),
+                in_=x_scales[:, 4 * q : 4 * q + 4, :].bitcast(I32),
+            )
+        w1_pass1_raw = []
         for s in range(2):
-            w11_raw.append(sb("w11_raw%d" % s, [P, PACK, H // 2], F32))
-            nc.sync.dma_start(out=w11_raw[s][:], in_=w1_rows[1][:, :, s * (H // 2) : (s + 1) * (H // 2)])
+            w1_pass1_raw.append(sb("w1_pass1_raw%d" % s, [P, PACK, H // 2], F32))
+            nc.sync.dma_start(out=w1_pass1_raw[s][:], in_=w1_rows[1][:, :, s * (H // 2) : (s + 1) * (H // 2)])
         x_codes = []
         for g in range(2):
             x_codes.append(sb("x_codes%d" % g, [P, T], U32))
-            nc.sync.dma_start(out=x_codes[g][:].bitcast(I32), in_=x_words[g].rearrange("p n t -> p (n t)").bitcast(I32))
+            nc.sync.dma_start(out=x_codes[g][:].bitcast(I32), in_=x_words[g].rearrange("p n j -> p (n j)").bitcast(I32))
         nc.sync.dma_start(lists[0][:], pos1)
         nc.sync.dma_start(lists[1][:], pos2)
-        a_raw = []
+        a_rows = aT.rearrange("(p j) (d v) -> p j d v", j=PACK, d=D)
+        a_late = []
         for d in range(D):
-            a_raw.append(sb("a_raw%d" % d, [P, PACK, HALF], F32))
-            nc.sync.dma_start(out=a_raw[d][:], in_=a_rows[:, :, d, HALF:])
-        for q in range(4):
-            nc.sync.dma_start(
-                out=w2_sc_raw[32 * q : 32 * q + 4, :].bitcast(I32),
-                in_=w2_scales[0, 4 * q : 4 * q + 4, :].bitcast(I32),
-            )
+            a_late.append(sb("a_late%d" % d, [P, PACK, HALF], F32))
+            nc.sync.dma_start(out=a_late[d][:], in_=a_rows[:, :, d, HALF:])
 
         w2_codes = sb("w2_codes", [P, 2 * H], U8)
         nc.vector.tensor_copy(
@@ -86,199 +92,192 @@ def tile_picked_wdime_none_lo_kernel(tc, x_words, x_scales, aT, w1, w3, w2_words
             in_=w2_raw[:].rearrange("p (m t b) -> p m t b", t=PACK, b=2),
         )
 
-        def cast_a(name, raw, width, copy, tag=None):
-            grouped = sb(name, [P, width * PACK], BF16, tag)
+        def weave(name, rows, width, copy, bytes_of=None):
+            woven = sb(name, [P, width * PACK], BF16, bytes_of)
             copy(
-                out=grouped[:].rearrange("p (c i j) -> p c j i", i=4, j=PACK),
-                in_=raw.rearrange("p j (c i) -> p c j i", i=4),
+                out=woven[:].rearrange("p (c i j) -> p c j i", i=LINE, j=PACK),
+                in_=rows.rearrange("p j (c i) -> p c j i", i=LINE),
             )
-            return grouped
+            return woven
 
-        def quantise(name, grouped, width):
+        def dealt_views(woven, raw, m0):
+            src = raw[:].rearrange("p j (m t) -> p m j t", t=PACK)
+            dst = woven[:].rearrange("p (t m j) -> p m j t", t=PACK, j=PACK)[:, m0 : m0 + src.shape[1]]
+            return dst, src
+
+        def quantise(name, woven, width):
             codes = sb(name + "_codes", [P, width], U32)
             scales = sb(name + "_scales", [P, width], U8)
-            nc.vector.quantize_mx(out=codes[:].bitcast(FP8X4), scales=scales[:], in_=grouped)
+            nc.vector.quantize_mx(out=codes[:].bitcast(FP8X4), scales=scales[:], in_=woven)
             return codes, scales
 
-        def cast_w(grouped, raw, m0, count):
-            dst = grouped[:].rearrange("p (t m j) -> p m j t", t=PACK, j=PACK)[:, m0 : m0 + count]
-            src = raw[:].rearrange("p j (m t) -> p m j t", t=PACK)
-            share = count * V_SHARE // P // 4 * 4
-            nc.vector.tensor_copy(out=dst[:, :share], in_=src[:, :share])
-            nc.scalar.copy(out=dst[:, share:], in_=src[:, share:])
+        filters = {}
 
-        filt = {}
-
-        def filter_product(dst, t, a_q):
+        def filter_product(dst, t, a_mx):
             cols = slice(t * P, (t + 1) * P)
             nc.tensor.matmul_mx(
                 out=dst,
-                lhsT=w3_q[0][:, cols].bitcast(FP8X4),
-                lhsT_scale=w3_q[1][:, cols],
-                rhs=a_q[0][:].bitcast(FP8X4),
-                rhs_scale=a_q[1][:],
+                lhsT=w3_mx[0][:, cols].bitcast(FP8X4),
+                lhsT_scale=w3_mx[1][:, cols],
+                rhs=a_mx[0][:].bitcast(FP8X4),
+                rhs_scale=a_mx[1][:],
                 start=True,
                 stop=True,
             )
 
-        def late_filters(d, a_q):
+        def late_filters(d, a_mx):
             for pair in range(2):
-                bank = psum.tile([P, 2, HALF], F32, name="f_bank", tag="b%d" % (2 * d + pair))
+                bank = bank_tile("late_filter_bank", [P, 2, HALF], 2 * d + pair)
                 for e in range(2):
-                    filter_product(bank[:, e, :], 2 * pair + e, a_q)
-                both = sb("filt_late%d%d" % (d, pair), [P, 2, HALF], F32)
-                nc.scalar.copy(out=both[:], in_=bank[:])
+                    filter_product(bank[:, e, :], 2 * pair + e, a_mx)
+                both_slots = sb("late_filters%d%d" % (d, pair), [P, 2, HALF], F32)
+                nc.scalar.copy(out=both_slots[:], in_=bank[:])
                 for e in range(2):
-                    filt[d, 1, 2 * pair + e] = both[:, e, :]
+                    filters[d, 1, 2 * pair + e] = both_slots[:, e, :]
 
-        a_first_bf = cast_a("a_first_bf", a_first[:].rearrange("p (j d) v -> p j (d v)", d=D), T, nc.vector.tensor_copy)
-        a_first_q = quantise("a_first", a_first_bf[:], T)
-        w3_bf = sb("w3_bf", [P, H * PACK], BF16)
-        cast_w(w3_bf, w3_raw, 0, P)
-        w3_q = quantise("w3", w3_bf[:], H)
-        f_banks = []
+        a_first_woven = weave("a_first_woven", a_first[:].rearrange("p (j d) v -> p j (d v)", d=D), T, nc.vector.tensor_copy)
+        a_first_mx = quantise("a_first", a_first_woven[:], T)
+        w2_dealt_scales = sb("w2_dealt_scales", [P, H], U8)
+        nc.vector.tensor_copy(
+            out=w2_dealt_scales[:].rearrange("p (t m) -> p m t", t=PACK),
+            in_=w2_scale_rows[:].rearrange("p (m t) -> p m t", t=PACK),
+        )
+        w3_woven = sb("w3_woven", [P, H * PACK], BF16)
+        dst, src = dealt_views(w3_woven, w3_raw, 0)
+        nc.vector.tensor_copy(out=dst[:, :W3_ON_VECTOR], in_=src[:, :W3_ON_VECTOR])
+        nc.scalar.copy(out=dst[:, W3_ON_VECTOR:], in_=src[:, W3_ON_VECTOR:])
+        w3_mx = quantise("w3", w3_woven[:], H)
+        first_filter_banks = []
         for t in range(PACK):
-            f_banks.append(psum.tile([P, T], F32, name="f_first", tag="b%d" % t))
-            filter_product(f_banks[t][:], t, a_first_q)
-        w10_bf = sb("w10_bf", [P, H * PACK], BF16)
-        cast_w(w10_bf, w10_raw, 0, P)
-        w10_q = quantise("w10", w10_bf[:], H)
-        w11_bf = sb("w11_bf", [P, H * PACK], BF16, "w10_bf")
+            first_filter_banks.append(bank_tile("first_filter_bank", [P, T], t))
+            filter_product(first_filter_banks[t][:], t, a_first_mx)
+        w1_pass0_woven = sb("w1_pass0_woven", [P, H * PACK], BF16)
+        nc.vector.tensor_copy(*dealt_views(w1_pass0_woven, w1_pass0_raw, 0))
+        w1_pass0_mx = quantise("w1_pass0", w1_pass0_woven[:], H)
+        w1_pass1_woven = sb("w1_pass1_woven", [P, H * PACK], BF16, "w1_pass0_woven")
         for s in range(2):
-            cast_w(w11_bf, w11_raw[s], s * (P // 2), P // 2)
-        w11_q = [quantise("w11%d" % u, w11_bf[:, u * 2 * K_PASS : (u + 1) * 2 * K_PASS], 2 * P) for u in range(2)]
+            nc.vector.tensor_copy(*dealt_views(w1_pass1_woven, w1_pass1_raw[s], s * (P // 2)))
+        w1_pass1_mx = [quantise("w1_pass1_slot%d" % t, w1_pass1_woven[:, t * K_PASS : (t + 1) * K_PASS], P) for t in range(PACK)]
 
         hidden = []
         for t in range(PACK):
-            both = sb("filt_first%d" % t, [P, D, HALF], F32)
-            nc.scalar.copy(out=both[:].rearrange("p d v -> p (d v)"), in_=f_banks[t][:])
+            both_lists = sb("first_filters%d" % t, [P, D, HALF], F32)
+            nc.scalar.copy(out=both_lists[:].rearrange("p d v -> p (d v)"), in_=first_filter_banks[t][:])
             for d in range(D):
-                filt[d, 0, t] = both[:, d, :]
-            bank = psum.tile([P, T], F32, name="h_bank", tag="b%d" % (4 + t))
-            stationary = ((w10_q, slice(t * P, (t + 1) * P)), (w11_q[t // 2], slice(t % 2 * P, (t % 2 + 1) * P)))
+                filters[d, 0, t] = both_lists[:, d, :]
+            bank = bank_tile("hidden_bank", [P, T], PACK + t)
+            stationary = ((w1_pass0_mx, slice(t * P, (t + 1) * P)), (w1_pass1_mx[t], slice(0, P)))
             order = (0, 1) if t == 0 else (1, 0)
             for g in order:
-                w_q, cols = stationary[g]
+                w_mx, cols = stationary[g]
                 nc.tensor.matmul_mx(
                     out=bank[:],
-                    lhsT=w_q[0][:, cols].bitcast(FP8X4),
-                    lhsT_scale=w_q[1][:, cols],
+                    lhsT=w_mx[0][:, cols].bitcast(FP8X4),
+                    lhsT_scale=w_mx[1][:, cols],
                     rhs=x_codes[g][:].bitcast(FP8X4),
-                    rhs_scale=x_sc[4 * g :, :],
+                    rhs_scale=x_scale_rows[4 * g :, :],
                     start=(g == order[0]),
                     stop=(g == order[1]),
                 )
             hidden.append(sb("hidden%d" % t, [P, T], F32))
-            nc.scalar.activation(hidden[t][:], bank[:], SILU)
+            nc.scalar.activation(hidden[t][:], bank[:], SILU, bias=zero_bias[:])
 
-        probe = sb("probe", [P, 2], F32)
-        nc.gpsimd.tensor_copy(out=probe[:, 0:1], in_=hidden[0][:, 0:1])
-
-        def gather(d, t, v0, width, dst):
+        def gather(d, t, v0, width, terms):
             half, off = divmod(v0, HALF)
             nc.vector.tensor_tensor(
-                dst[:, t, :],
+                terms[:, t, :],
                 hidden[t][:].indirect(lists[d][:, v0 // 16 : (v0 + width) // 16]),
-                filt[d, half, t][:, off : off + width],
+                filters[d, half, t][:, off : off + width],
                 MULT,
             )
 
-        def add_terms(name, first, second, width, tag=None):
-            grouped = sb(name, [P, width * PACK], BF16, tag)
+        def add_terms(name, first, second, width, bytes_of=None):
+            woven = sb(name, [P, width * PACK], BF16, bytes_of)
             nc.vector.tensor_tensor(
-                grouped[:].rearrange("p (c i t) -> p c t i", i=4, t=PACK),
-                first.rearrange("p t (c i) -> p c t i", i=4),
-                second.rearrange("p t (c i) -> p c t i", i=4),
+                woven[:].rearrange("p (c i t) -> p c t i", i=LINE, t=PACK),
+                first.rearrange("p t (c i) -> p c t i", i=LINE),
+                second.rearrange("p t (c i) -> p c t i", i=LINE),
                 ADD,
             )
-            return grouped
+            return woven
 
         y_codes = sb("y_codes", [P, T], U32)
         y_scales = sb("y_scales", [P, T], U8)
         out_rows = out_0.rearrange("(p t) v -> p t v", t=PACK)
         out_words = out_1[0].rearrange("p n t -> p (n t)").bitcast(I32)
 
-        def project(z_q, off, dst, t):
+        def project(z_mx, off, dst, t):
             nc.tensor.matmul_mx(
                 out=dst,
                 lhsT=w2_codes[:, 2 * P * t : 2 * P * (t + 1)].bitcast(FP4X4),
-                lhsT_scale=w2_sc[:, P * t : P * (t + 1)],
-                rhs=z_q[0][:, off : off + QUART].bitcast(FP8X4),
-                rhs_scale=z_q[1][:, off : off + QUART],
+                lhsT_scale=w2_dealt_scales[:, P * t : P * (t + 1)],
+                rhs=z_mx[0][:, off : off + QUARTER].bitcast(FP8X4),
+                rhs_scale=z_mx[1][:, off : off + QUARTER],
                 start=True,
                 stop=True,
             )
 
-        def quantise_y(grouped, v0, width):
+        def project_and_store(z_mx, off, v0, number):
+            bank = bank_tile("y_bank", [P, PACK, QUARTER], number)
+            for t in range(PACK):
+                project(z_mx, off, bank[:, t, :], t)
+            y = sb("y%d" % v0, [P, PACK, QUARTER], F32)
+            nc.scalar.copy(out=y[:], in_=bank[:])
+            nc.sync.dma_start(out=out_rows[:, :, v0 : v0 + QUARTER], in_=y[:])
+            return bank, y
+
+        def quantise_y(woven, v0, width):
             cols = slice(v0, v0 + width)
-            nc.vector.quantize_mx(out=y_codes[:, cols].bitcast(FP8X4), scales=y_scales[:, cols], in_=grouped[:])
+            nc.vector.quantize_mx(out=y_codes[:, cols].bitcast(FP8X4), scales=y_scales[:, cols], in_=woven[:])
             nc.sync.dma_start(out=out_words[:, cols], in_=y_codes[:, cols].bitcast(I32))
 
-        def finish_scalar(z_q, off, v0, y_bf, tag):
-            bank = psum.tile([P, PACK, QUART], F32, name="y_bank", tag=tag)
-            for t in range(PACK):
-                project(z_q, off, bank[:, t, :], t)
-            y = sb("y%d" % v0, [P, PACK, QUART], F32)
-            nc.scalar.copy(out=y[:], in_=bank[:])
-            nc.sync.dma_start(out=out_rows[:, :, v0 : v0 + QUART], in_=y[:])
-            nc.scalar.copy(out=y_bf.rearrange("p (v t) -> p v t", t=PACK), in_=bank[:].rearrange("p t v -> p v t"))
-
-        term = {}
-        for d in range(D):
-            term[d, 0] = sb("term%d0" % d, [P, PACK, HALF], F32)
+        first_terms = [sb("first_terms%d" % d, [P, PACK, HALF], F32) for d in range(D)]
         for t in range(PACK):
             for d in range(D):
-                gather(d, t, 0, HALF, term[d, 0])
-        a0_bf = cast_a("a0_bf", a_raw[0][:], HALF, nc.scalar.copy, "w111_codes")
-        late_filters(0, quantise("a0", a0_bf[:], HALF))
-        a1_bf = cast_a("a1_bf", a_raw[1][:], HALF, nc.scalar.copy, "a_raw0")
-        z0_bf = add_terms("z0_bf", term[0, 0][:], term[1, 0][:], HALF, "w111_codes")
-        late_filters(1, quantise("a1", a1_bf[:], HALF))
-        w2_sc = sb("w2_sc", [P, H], U8, "filt_first3")
-        nc.vector.tensor_copy(
-            out=w2_sc[:].rearrange("p (t m) -> p m t", t=PACK),
-            in_=w2_sc_raw[:].rearrange("p (m t) -> p m t", t=PACK),
-        )
-        z0_q = quantise("z0", z0_bf[:], HALF)
+                gather(d, t, 0, HALF, first_terms[d])
+        a_late0_woven = weave("a_late0_woven", a_late[0][:], HALF, nc.scalar.copy, "w1_pass1_slot1_codes")
+        late_filters(0, quantise("a_late0", a_late0_woven[:], HALF))
+        a_late1_woven = weave("a_late1_woven", a_late[1][:], HALF, nc.scalar.copy, "a_late0")
+        z_first_woven = add_terms("z_first_woven", first_terms[0][:], first_terms[1][:], HALF, "w1_pass1_slot1_codes")
+        late_filters(1, quantise("a_late1", a_late1_woven[:], HALF))
+        z_first_mx = quantise("z_first", z_first_woven[:], HALF)
 
-        probe2 = sb("probe2", [P, 2], U32)
-        nc.gpsimd.tensor_copy(out=probe2[:, 0:1], in_=z0_q[0][:, 0:1])
-        term[0, 1] = sb("term01", [P, PACK, HALF], F32)
+        late_terms = sb("late_terms", [P, PACK, HALF], F32)
         for t in range(PACK):
-            gather(0, t, HALF, HALF, term[0, 1])
-        y0_bf = sb("y0_bf", [P, HALF * PACK], BF16)
+            gather(0, t, HALF, HALF, late_terms)
+        y_first_woven = sb("y_first_woven", [P, HALF * PACK], BF16)
         for k in range(2):
-            finish_scalar(z0_q, k * QUART, k * QUART, y0_bf[:, k * QUART * PACK : (k + 1) * QUART * PACK], "b%d" % (2 + k))
-        term2 = sb("term12", [P, PACK, QUART], F32)
-        term3 = sb("term13", [P, PACK, QUART], F32)
+            bank = project_and_store(z_first_mx, k * QUARTER, k * QUARTER, 2 + k)[0]
+            nc.scalar.copy(
+                out=y_first_woven[:, k * K_PASS : (k + 1) * K_PASS].rearrange("p (v t) -> p v t", t=PACK),
+                in_=bank[:].rearrange("p t v -> p v t"),
+            )
+        third_terms = sb("third_terms", [P, PACK, QUARTER], F32)
+        last_terms = sb("last_terms", [P, PACK, QUARTER], F32)
         for t in range(PACK):
-            gather(1, t, 2 * QUART, QUART, term2)
-        gather(1, 0, 3 * QUART, QUART, term3)
-        z2_bf = add_terms("z2_bf", term[0, 1][:, :, :QUART], term2[:], QUART)
-        gather(1, 1, 3 * QUART, QUART, term3)
-        z2_q = quantise("z2", z2_bf[:], QUART)
-        gather(1, 2, 3 * QUART, QUART, term3)
-        gather(1, 3, 3 * QUART, QUART, term3)
-        quantise_y(y0_bf, 0, HALF)
-        z3_bf = add_terms("z3_bf", term[0, 1][:, :, QUART:], term3[:], QUART)
-        y2_bf = sb("y2_bf", [P, QUART * PACK], BF16)
-        finish_scalar(z2_q, 0, 2 * QUART, y2_bf[:], "b4")
-        z3_q = quantise("z3", z3_bf[:], QUART)
-        quantise_y(y2_bf, 2 * QUART, QUART)
+            gather(1, t, 2 * QUARTER, QUARTER, third_terms)
+        gather(1, 0, 3 * QUARTER, QUARTER, last_terms)
+        z_third_woven = add_terms("z_third_woven", late_terms[:, :, :QUARTER], third_terms[:], QUARTER)
+        gather(1, 1, 3 * QUARTER, QUARTER, last_terms)
+        z_third_mx = quantise("z_third", z_third_woven[:], QUARTER)
+        gather(1, 2, 3 * QUARTER, QUARTER, last_terms)
+        gather(1, 3, 3 * QUARTER, QUARTER, last_terms)
+        z_last_woven = add_terms("z_last_woven", late_terms[:, :, QUARTER:], last_terms[:], QUARTER)
+        y_third = project_and_store(z_third_mx, 0, 2 * QUARTER, PACK)[1]
+        z_last_mx = quantise("z_last", z_last_woven[:], QUARTER)
+        y_third_woven = weave("y_third_woven", y_third[:], QUARTER, nc.vector.tensor_copy, "z_last_woven")
+        quantise_y(y_first_woven, 0, HALF)
+        quantise_y(y_third_woven, 2 * QUARTER, QUARTER)
 
-        y3 = sb("y3", [P, PACK, QUART], F32)
+        y_last = sb("y_last", [P, PACK, QUARTER], F32)
         for pair, copy in enumerate((nc.vector.tensor_copy, nc.scalar.copy)):
-            bank = psum.tile([P, 2, QUART], F32, name="last_bank", tag="b%d" % (5 + pair))
+            bank = bank_tile("last_bank", [P, 2, QUARTER], PACK + 1 + pair)
             for e in range(2):
-                project(z3_q, 0, bank[:, e, :], 2 * pair + e)
-            copy(out=y3[:, 2 * pair : 2 * pair + 2, :], in_=bank[:])
-        nc.sync.dma_start(out=out_rows[:, :, 3 * QUART :], in_=y3[:])
-        y3_bf = sb("y3_bf", [P, QUART * PACK], BF16)
-        nc.vector.tensor_copy(
-            out=y3_bf[:].rearrange("p (c i t) -> p c t i", i=4, t=PACK),
-            in_=y3[:].rearrange("p t (c i) -> p c t i", i=4),
-        )
-        quantise_y(y3_bf, 3 * QUART, QUART)
+                project(z_last_mx, 0, bank[:, e, :], 2 * pair + e)
+            copy(out=y_last[:, 2 * pair : 2 * pair + 2, :], in_=bank[:])
+        nc.sync.dma_start(out=out_rows[:, :, 3 * QUARTER :], in_=y_last[:])
+        y_last_woven = weave("y_last_woven", y_last[:], QUARTER, nc.vector.tensor_copy)
+        quantise_y(y_last_woven, 3 * QUARTER, QUARTER)
         for q, queue in enumerate((nc.scalar, nc.sync, nc.scalar, nc.sync)):
             queue.dma_start(
                 out=out_2[0, 4 * q : 4 * q + 4, :].bitcast(I32),

from contextlib import ExitStack

import concourse.mybir as mybir

K, T, H, J, D = 1024, 512, 512, 512, 2
FLOPS = 2 * (K * H * T + J * H * D * T + H * H * T)

F32 = mybir.dt.float32
BF16 = mybir.dt.bfloat16
I32 = mybir.dt.int32
U32 = mybir.dt.uint32
U16 = mybir.dt.uint16
U8 = mybir.dt.uint8
FP8X4 = mybir.dt.float8_e4m3fn_x4
FP4X4 = mybir.dt.float4_e2m1fn_x4
MULT = mybir.AluOpType.mult
ADD = mybir.AluOpType.add
SILU = mybir.ActivationFunctionType.Silu

P = 128
PACK = 4
K_PASS = P * PACK
QUADRANTS = 4
HALF = T // 2
QUARTER = T // 4
LINE = 4
W3_ON_VECTOR = 84


def tile_picked_wdime_none_lo_kernel(tc, x_words, x_scales, aT, w1, w3, w2_words, w2_scales, pos1, pos2, out_0, out_1, out_2):
    nc = tc.nc
    with ExitStack() as ctx:
        keep = ctx.enter_context(tc.tile_pool(name="keep", bufs=1))
        psum = ctx.enter_context(tc.psum_pool(name="psum", bufs=1))

        def sb(name, shape, dtype, bytes_of=None):
            return keep.tile(shape, dtype, name=name, tag=bytes_of or name, align_bytes=64)

        def bank_tile(name, shape, number):
            return psum.tile(shape, F32, name=name, tag="bank%d" % number)

        lists = [keep.tile([P, T // 16], U16, name="list%d" % d) for d in range(D)]

        zero = sb("zero", [P, 1], F32)
        zero_bias = sb("zero_bias", [P, 1], F32)
        nc.vector.memset(zero[:], 0.0)

        x_scale_rows = sb("x_scale_rows", [P, T], U8)
        w2_scale_rows = sb("w2_scale_rows", [P, H], U8)
        nc.gpsimd.memset(w2_scale_rows[:].bitcast(I32), 0)
        nc.gpsimd.memset(x_scale_rows[:].bitcast(I32), 0)
        nc.scalar.activation(zero_bias[:], zero[:], SILU)

        w2_raw = sb("w2_raw", [P, 2 * H], U8)
        nc.sync.dma_start(out=w2_raw[:].bitcast(I32), in_=w2_words[0].bitcast(I32))
        a_first = sb("a_first", [P, PACK * D, HALF], F32)
        nc.sync.dma_start(out=a_first[:], in_=aT.rearrange("(p j) (d v) -> p (j d) v", j=PACK, d=D)[:, :, :HALF])
        for q in range(QUADRANTS):
            nc.sync.dma_start(
                out=w2_scale_rows[32 * q : 32 * q + 4, :].bitcast(I32),
                in_=w2_scales[0, 4 * q : 4 * q + 4, :].bitcast(I32),
            )
        w3_raw = sb("w3_raw", [P, PACK, H], F32)
        nc.sync.dma_start(out=w3_raw[:], in_=w3.rearrange("(p j) c -> p j c", j=PACK))
        w1_rows = w1.rearrange("(g p j) c -> g p j c", g=2, j=PACK)
        w1_pass0_raw = sb("w1_pass0_raw", [P, PACK, H], F32)
        nc.sync.dma_start(out=w1_pass0_raw[:], in_=w1_rows[0])
        for q in range(QUADRANTS):
            nc.sync.dma_start(
                out=x_scale_rows[32 * q : 32 * q + 8, :].bitcast(I32),
                in_=x_scales[:, 4 * q : 4 * q + 4, :].bitcast(I32),
            )
        w1_pass1_raw = []
        for s in range(2):
            w1_pass1_raw.append(sb("w1_pass1_raw%d" % s, [P, PACK, H // 2], F32))
            nc.sync.dma_start(out=w1_pass1_raw[s][:], in_=w1_rows[1][:, :, s * (H // 2) : (s + 1) * (H // 2)])
        x_codes = []
        for g in range(2):
            x_codes.append(sb("x_codes%d" % g, [P, T], U32))
            nc.sync.dma_start(out=x_codes[g][:].bitcast(I32), in_=x_words[g].rearrange("p n j -> p (n j)").bitcast(I32))
        nc.sync.dma_start(lists[0][:], pos1)
        nc.sync.dma_start(lists[1][:], pos2)
        a_rows = aT.rearrange("(p j) (d v) -> p j d v", j=PACK, d=D)
        a_late = []
        for d in range(D):
            a_late.append(sb("a_late%d" % d, [P, PACK, HALF], F32))
            nc.sync.dma_start(out=a_late[d][:], in_=a_rows[:, :, d, HALF:])

        w2_codes = sb("w2_codes", [P, 2 * H], U8)
        nc.vector.tensor_copy(
            out=w2_codes[:].rearrange("p (t m b) -> p m t b", t=PACK, b=2),
            in_=w2_raw[:].rearrange("p (m t b) -> p m t b", t=PACK, b=2),
        )

        def weave(name, rows, width, copy, bytes_of=None):
            woven = sb(name, [P, width * PACK], BF16, bytes_of)
            copy(
                out=woven[:].rearrange("p (c i j) -> p c j i", i=LINE, j=PACK),
                in_=rows.rearrange("p j (c i) -> p c j i", i=LINE),
            )
            return woven

        def dealt_views(woven, raw, m0):
            src = raw[:].rearrange("p j (m t) -> p m j t", t=PACK)
            dst = woven[:].rearrange("p (t m j) -> p m j t", t=PACK, j=PACK)[:, m0 : m0 + src.shape[1]]
            return dst, src

        def quantise(name, woven, width):
            codes = sb(name + "_codes", [P, width], U32)
            scales = sb(name + "_scales", [P, width], U8)
            nc.vector.quantize_mx(out=codes[:].bitcast(FP8X4), scales=scales[:], in_=woven)
            return codes, scales

        filters = {}

        def filter_product(dst, t, a_mx):
            cols = slice(t * P, (t + 1) * P)
            nc.tensor.matmul_mx(
                out=dst,
                lhsT=w3_mx[0][:, cols].bitcast(FP8X4),
                lhsT_scale=w3_mx[1][:, cols],
                rhs=a_mx[0][:].bitcast(FP8X4),
                rhs_scale=a_mx[1][:],
                start=True,
                stop=True,
            )

        def late_filters(d, a_mx):
            for pair in range(2):
                bank = bank_tile("late_filter_bank", [P, 2, HALF], 2 * d + pair)
                for e in range(2):
                    filter_product(bank[:, e, :], 2 * pair + e, a_mx)
                both_slots = sb("late_filters%d%d" % (d, pair), [P, 2, HALF], F32)
                nc.scalar.copy(out=both_slots[:], in_=bank[:])
                for e in range(2):
                    filters[d, 1, 2 * pair + e] = both_slots[:, e, :]

        a_first_woven = weave("a_first_woven", a_first[:].rearrange("p (j d) v -> p j (d v)", d=D), T, nc.vector.tensor_copy)
        a_first_mx = quantise("a_first", a_first_woven[:], T)
        w2_dealt_scales = sb("w2_dealt_scales", [P, H], U8)
        nc.vector.tensor_copy(
            out=w2_dealt_scales[:].rearrange("p (t m) -> p m t", t=PACK),
            in_=w2_scale_rows[:].rearrange("p (m t) -> p m t", t=PACK),
        )
        w3_woven = sb("w3_woven", [P, H * PACK], BF16)
        dst, src = dealt_views(w3_woven, w3_raw, 0)
        nc.vector.tensor_copy(out=dst[:, :W3_ON_VECTOR], in_=src[:, :W3_ON_VECTOR])
        nc.scalar.copy(out=dst[:, W3_ON_VECTOR:], in_=src[:, W3_ON_VECTOR:])
        w3_mx = quantise("w3", w3_woven[:], H)
        first_filter_banks = []
        for t in range(PACK):
            first_filter_banks.append(bank_tile("first_filter_bank", [P, T], t))
            filter_product(first_filter_banks[t][:], t, a_first_mx)
        w1_pass0_woven = sb("w1_pass0_woven", [P, H * PACK], BF16)
        nc.vector.tensor_copy(*dealt_views(w1_pass0_woven, w1_pass0_raw, 0))
        w1_pass0_mx = quantise("w1_pass0", w1_pass0_woven[:], H)
        w1_pass1_woven = sb("w1_pass1_woven", [P, H * PACK], BF16, "w1_pass0_woven")
        for s in range(2):
            nc.vector.tensor_copy(*dealt_views(w1_pass1_woven, w1_pass1_raw[s], s * (P // 2)))
        w1_pass1_mx = [quantise("w1_pass1_slot%d" % t, w1_pass1_woven[:, t * K_PASS : (t + 1) * K_PASS], P) for t in range(PACK)]

        hidden = []
        for t in range(PACK):
            both_lists = sb("first_filters%d" % t, [P, D, HALF], F32)
            nc.scalar.copy(out=both_lists[:].rearrange("p d v -> p (d v)"), in_=first_filter_banks[t][:])
            for d in range(D):
                filters[d, 0, t] = both_lists[:, d, :]
            bank = bank_tile("hidden_bank", [P, T], PACK + t)
            stationary = ((w1_pass0_mx, slice(t * P, (t + 1) * P)), (w1_pass1_mx[t], slice(0, P)))
            order = (0, 1) if t == 0 else (1, 0)
            for g in order:
                w_mx, cols = stationary[g]
                nc.tensor.matmul_mx(
                    out=bank[:],
                    lhsT=w_mx[0][:, cols].bitcast(FP8X4),
                    lhsT_scale=w_mx[1][:, cols],
                    rhs=x_codes[g][:].bitcast(FP8X4),
                    rhs_scale=x_scale_rows[4 * g :, :],
                    start=(g == order[0]),
                    stop=(g == order[1]),
                )
            hidden.append(sb("hidden%d" % t, [P, T], F32))
            nc.scalar.activation(hidden[t][:], bank[:], SILU, bias=zero_bias[:])

        def gather(d, t, v0, width, terms):
            half, off = divmod(v0, HALF)
            nc.vector.tensor_tensor(
                terms[:, t, :],
                hidden[t][:].indirect(lists[d][:, v0 // 16 : (v0 + width) // 16]),
                filters[d, half, t][:, off : off + width],
                MULT,
            )

        def add_terms(name, first, second, width, bytes_of=None):
            woven = sb(name, [P, width * PACK], BF16, bytes_of)
            nc.vector.tensor_tensor(
                woven[:].rearrange("p (c i t) -> p c t i", i=LINE, t=PACK),
                first.rearrange("p t (c i) -> p c t i", i=LINE),
                second.rearrange("p t (c i) -> p c t i", i=LINE),
                ADD,
            )
            return woven

        y_codes = sb("y_codes", [P, T], U32)
        y_scales = sb("y_scales", [P, T], U8)
        out_rows = out_0.rearrange("(p t) v -> p t v", t=PACK)
        out_words = out_1[0].rearrange("p n t -> p (n t)").bitcast(I32)

        def project(z_mx, off, dst, t):
            nc.tensor.matmul_mx(
                out=dst,
                lhsT=w2_codes[:, 2 * P * t : 2 * P * (t + 1)].bitcast(FP4X4),
                lhsT_scale=w2_dealt_scales[:, P * t : P * (t + 1)],
                rhs=z_mx[0][:, off : off + QUARTER].bitcast(FP8X4),
                rhs_scale=z_mx[1][:, off : off + QUARTER],
                start=True,
                stop=True,
            )

        def project_and_store(z_mx, off, v0, number):
            bank = bank_tile("y_bank", [P, PACK, QUARTER], number)
            for t in range(PACK):
                project(z_mx, off, bank[:, t, :], t)
            y = sb("y%d" % v0, [P, PACK, QUARTER], F32)
            nc.scalar.copy(out=y[:], in_=bank[:])
            nc.sync.dma_start(out=out_rows[:, :, v0 : v0 + QUARTER], in_=y[:])
            return bank, y

        def quantise_y(woven, v0, width):
            cols = slice(v0, v0 + width)
            nc.vector.quantize_mx(out=y_codes[:, cols].bitcast(FP8X4), scales=y_scales[:, cols], in_=woven[:])
            nc.sync.dma_start(out=out_words[:, cols], in_=y_codes[:, cols].bitcast(I32))

        first_terms = [sb("first_terms%d" % d, [P, PACK, HALF], F32) for d in range(D)]
        for t in range(PACK):
            for d in range(D):
                gather(d, t, 0, HALF, first_terms[d])
        a_late0_woven = weave("a_late0_woven", a_late[0][:], HALF, nc.scalar.copy, "w1_pass1_slot1_codes")
        late_filters(0, quantise("a_late0", a_late0_woven[:], HALF))
        a_late1_woven = weave("a_late1_woven", a_late[1][:], HALF, nc.scalar.copy, "a_late0")
        z_first_woven = add_terms("z_first_woven", first_terms[0][:], first_terms[1][:], HALF, "w1_pass1_slot1_codes")
        late_filters(1, quantise("a_late1", a_late1_woven[:], HALF))
        z_first_mx = quantise("z_first", z_first_woven[:], HALF)

        late_terms = sb("late_terms", [P, PACK, HALF], F32)
        for t in range(PACK):
            gather(0, t, HALF, HALF, late_terms)
        y_first_woven = sb("y_first_woven", [P, HALF * PACK], BF16)
        for k in range(2):
            bank = project_and_store(z_first_mx, k * QUARTER, k * QUARTER, 2 + k)[0]
            nc.scalar.copy(
                out=y_first_woven[:, k * K_PASS : (k + 1) * K_PASS].rearrange("p (v t) -> p v t", t=PACK),
                in_=bank[:].rearrange("p t v -> p v t"),
            )
        third_terms = sb("third_terms", [P, PACK, QUARTER], F32)
        last_terms = sb("last_terms", [P, PACK, QUARTER], F32)
        for t in range(PACK):
            gather(1, t, 2 * QUARTER, QUARTER, third_terms)
        gather(1, 0, 3 * QUARTER, QUARTER, last_terms)
        z_third_woven = add_terms("z_third_woven", late_terms[:, :, :QUARTER], third_terms[:], QUARTER)
        gather(1, 1, 3 * QUARTER, QUARTER, last_terms)
        z_third_mx = quantise("z_third", z_third_woven[:], QUARTER)
        gather(1, 2, 3 * QUARTER, QUARTER, last_terms)
        gather(1, 3, 3 * QUARTER, QUARTER, last_terms)
        z_last_woven = add_terms("z_last_woven", late_terms[:, :, QUARTER:], last_terms[:], QUARTER)
        y_third = project_and_store(z_third_mx, 0, 2 * QUARTER, PACK)[1]
        z_last_mx = quantise("z_last", z_last_woven[:], QUARTER)
        y_third_woven = weave("y_third_woven", y_third[:], QUARTER, nc.vector.tensor_copy, "z_last_woven")
        quantise_y(y_first_woven, 0, HALF)
        quantise_y(y_third_woven, 2 * QUARTER, QUARTER)

        y_last = sb("y_last", [P, PACK, QUARTER], F32)
        for pair, copy in enumerate((nc.vector.tensor_copy, nc.scalar.copy)):
            bank = bank_tile("last_bank", [P, 2, QUARTER], PACK + 1 + pair)
            for e in range(2):
                project(z_last_mx, 0, bank[:, e, :], 2 * pair + e)
            copy(out=y_last[:, 2 * pair : 2 * pair + 2, :], in_=bank[:])
        nc.sync.dma_start(out=out_rows[:, :, 3 * QUARTER :], in_=y_last[:])
        y_last_woven = weave("y_last_woven", y_last[:], QUARTER, nc.vector.tensor_copy)
        quantise_y(y_last_woven, 3 * QUARTER, QUARTER)
        for q, queue in enumerate((nc.scalar, nc.sync, nc.scalar, nc.sync)):
            queue.dma_start(
                out=out_2[0, 4 * q : 4 * q + 4, :].bitcast(I32),
                in_=y_scales[32 * q : 32 * q + 4, :].bitcast(I32),
            )
